import numpy as np
import ml_dtypes

BF16 = ml_dtypes.bfloat16


def bf(x):
    return np.asarray(x, np.float32).astype(BF16)


def f32(x):
    return np.asarray(x, np.float32)


def f64(x):
    return np.asarray(x).astype(np.float64)


def striped(idx):
    return np.tile(idx.reshape(-1, 16).T, (8, 1))


S, K, M, N, E, Q = 256, 128, 256, 512, 8, 64


def gelu_tanh(v):
    return 0.5 * v * (1.0 + np.tanh(np.sqrt(2.0 / np.pi) * (v + 0.044715 * v**3)))


def two_experts():
    first = np.random.permutation(S).reshape(E, S // E)
    return np.concatenate([np.random.permutation(np.concatenate([first[e], first[(e + 1) % E]])) for e in range(E)])


def setup_inputs():
    return {"table": bf(np.random.standard_normal((S, K))), "w": bf(np.random.standard_normal((E, K, M)) / np.sqrt(K)), "b": f32(0.5 * np.random.standard_normal((M, 1))), "offs": striped(two_experts())}


def reference(table, w, b, offs):
    idx = offs[:16].T.reshape(-1)
    x = f64(table)[idx].T
    y = np.concatenate([f64(w)[e].T @ x[:, e * Q : (e + 1) * Q] for e in range(E)], axis=1)
    return gelu_tanh(y + f64(b))

@@ -1,0 +1,58 @@
+import concourse.mybir as mybir
+from concourse.masks import make_identity
+
+P = 128
+S, K, M, N, E, Q = 256, 128, 256, 512, 8, 64
+TOKEN_BLOCKS = S // P
+OUT_BLOCKS = M // P
+OFFSET_COLUMNS = Q // 16
+EXPERTS_A_LOAD = E // 2
+
+BF16, F32, U16 = mybir.dt.bfloat16, mybir.dt.float32, mybir.dt.uint16
+GELU = mybir.ActivationFunctionType.Gelu_apprx_tanh
+
+FLOPS = 2 * K * M * N
+
+
+def tile_gather_matmul_kernel(tc, table, w, b, offs, out):
+    nc = tc.nc
+    with (
+        tc.tile_pool(name="held", bufs=1) as held,
+        tc.psum_pool(name="psum", bufs=1) as psum,
+    ):
+        offsets = held.tile([P, N // 16], U16, name="offsets")
+        nc.sync.dma_start(offsets[:], offs)
+
+        tokens = held.tile([P, TOKEN_BLOCKS, K], BF16, name="tokens")
+        nc.sync.dma_start(tokens[:], table.rearrange("(t p) k -> p t k", p=P))
+
+        weights = [held.tile([P, EXPERTS_A_LOAD, M], BF16, name=f"weights{h}") for h in range(2)]
+        w_by_k = w.rearrange("e k m -> k e m")
+        nc.scalar.dma_start(weights[0][:], w_by_k[:, 0:EXPERTS_A_LOAD, :])
+        nc.sync.dma_start(weights[1][:], w_by_k[:, EXPERTS_A_LOAD:E, :])
+
+        bias = held.tile([P, OUT_BLOCKS], F32, name="bias")
+        with nc.allow_non_contiguous_dma(reason="256 single float32 values, one to a partition"):
+            nc.scalar.dma_start(bias[:], b.rearrange("(a p) o -> p (a o)", p=P))
+
+        identity = held.tile([P, P], BF16, name="identity")
+        make_identity(nc, identity[:])
+        flipped = psum.tile([P, S], BF16, name="flipped")
+        for t in range(TOKEN_BLOCKS):
+            nc.tensor.transpose(flipped[:, t * P : (t + 1) * P], tokens[:, t, :], identity[:])
+        window = held.tile([P, S], BF16, name="window")
+        nc.vector.tensor_copy(window[:], flipped[:])
+
+        for a in range(OUT_BLOCKS):
+            y = psum.tile([P, N], F32, name=f"y{a}")
+            for e in range(E):
+                nc.tensor.matmul(
+                    y[:, e * Q : (e + 1) * Q],
+                    weights[e // EXPERTS_A_LOAD][:, e % EXPERTS_A_LOAD, a * P : (a + 1) * P],
+                    window[:].indirect(offsets[:, e * OFFSET_COLUMNS : (e + 1) * OFFSET_COLUMNS]),
+                    start=True,
+                    stop=True,
+                )
+            result = held.tile([P, N], F32, name=f"result{a}")
+            nc.scalar.activation(result[:], y[:], GELU, bias=bias[:, a : a + 1])
+            nc.sync.dma_start(out[a * P : (a + 1) * P, :], result[:])

@@ -6,7 +6,9 @@ S, K, M, N, E, Q = 256, 128, 256, 512, 8, 64
 TOKEN_BLOCKS = S // P
 OUT_BLOCKS = M // P
 OFFSET_COLUMNS = Q // 16
-EXPERTS_A_LOAD = E // 2
+EXPERT_GROUPS = 4
+GROUP = E // EXPERT_GROUPS
+GROUP_COLUMNS = GROUP * Q
 
 BF16, F32, U16 = mybir.dt.bfloat16, mybir.dt.float32, mybir.dt.uint16
 GELU = mybir.ActivationFunctionType.Gelu_apprx_tanh
@@ -19,40 +21,50 @@ def tile_gather_matmul_kernel(tc, table, w, b, offs, out):
     with (
         tc.tile_pool(name="held", bufs=1) as held,
         tc.psum_pool(name="psum", bufs=1) as psum,
+        tc.psum_pool(name="products", bufs=4) as products,
     ):
         offsets = held.tile([P, N // 16], U16, name="offsets")
         nc.sync.dma_start(offsets[:], offs)
 
         tokens = held.tile([P, TOKEN_BLOCKS, K], BF16, name="tokens")
-        nc.sync.dma_start(tokens[:], table.rearrange("(t p) k -> p t k", p=P))
+        nc.scalar.dma_start(tokens[:], table.rearrange("(t p) k -> p t k", p=P))
 
-        weights = [held.tile([P, EXPERTS_A_LOAD, M], BF16, name=f"weights{h}") for h in range(2)]
+        weights = [held.tile([P, GROUP, M], BF16, name=f"weights{g}") for g in range(EXPERT_GROUPS)]
         w_by_k = w.rearrange("e k m -> k e m")
-        nc.scalar.dma_start(weights[0][:], w_by_k[:, 0:EXPERTS_A_LOAD, :])
-        nc.sync.dma_start(weights[1][:], w_by_k[:, EXPERTS_A_LOAD:E, :])
+        for g in range(EXPERT_GROUPS):
+            nc.sync.dma_start(weights[g][:], w_by_k[:, g * GROUP : (g + 1) * GROUP, :])
 
         bias = held.tile([P, OUT_BLOCKS], F32, name="bias")
         with nc.allow_non_contiguous_dma(reason="256 single float32 values, one to a partition"):
             nc.scalar.dma_start(bias[:], b.rearrange("(a p) o -> p (a o)", p=P))
 
+        scratch = held.tile([P, 1], F32, name="scratch")
+        nc.vector.memset(scratch[:], 0.0)
+        nc.scalar.activation(scratch[:], scratch[:], GELU)
+
         identity = held.tile([P, P], BF16, name="identity")
         make_identity(nc, identity[:])
-        flipped = psum.tile([P, S], BF16, name="flipped")
-        for t in range(TOKEN_BLOCKS):
-            nc.tensor.transpose(flipped[:, t * P : (t + 1) * P], tokens[:, t, :], identity[:])
         window = held.tile([P, S], BF16, name="window")
-        nc.vector.tensor_copy(window[:], flipped[:])
+        flipped = [psum.tile([P, P], BF16, name=f"flipped{t}") for t in range(TOKEN_BLOCKS)]
+        for t in range(TOKEN_BLOCKS):
+            nc.tensor.transpose(flipped[t][:], tokens[:, t, :], identity[:])
+        nc.vector.tensor_copy(window[:, 0:P], flipped[0][:])
+        nc.scalar.copy(window[:, P:S], flipped[1][:])
 
-        for a in range(OUT_BLOCKS):
-            y = psum.tile([P, N], F32, name=f"y{a}")
-            for e in range(E):
-                nc.tensor.matmul(
-                    y[:, e * Q : (e + 1) * Q],
-                    weights[e // EXPERTS_A_LOAD][:, e % EXPERTS_A_LOAD, a * P : (a + 1) * P],
-                    window[:].indirect(offsets[:, e * OFFSET_COLUMNS : (e + 1) * OFFSET_COLUMNS]),
-                    start=True,
-                    stop=True,
+        for g in range(EXPERT_GROUPS):
+            for a in range(OUT_BLOCKS):
+                y = products.tile([P, GROUP_COLUMNS], F32, name="y")
+                for i in range(GROUP):
+                    e = g * GROUP + i
+                    nc.tensor.matmul(
+                        y[:, i * Q : (i + 1) * Q],
+                        weights[g][:, i, a * P : (a + 1) * P],
+                        window[:].indirect(offsets[:, e * OFFSET_COLUMNS : (e + 1) * OFFSET_COLUMNS]),
+                        start=True,
+                        stop=True,
+                    )
+                result = held.tile([P, GROUP_COLUMNS], F32, name=f"result{g}{a}")
+                nc.scalar.activation(result[:], y[:], GELU, bias=bias[:, a : a + 1])
+                nc.sync.dma_start(
+                    out[a * P : (a + 1) * P, g * GROUP_COLUMNS : (g + 1) * GROUP_COLUMNS], result[:]
                 )
-            result = held.tile([P, N], F32, name=f"result{a}")
-            nc.scalar.activation(result[:], y[:], GELU, bias=bias[:, a : a + 1])
-            nc.sync.dma_start(out[a * P : (a + 1) * P, :], result[:])

@@ -9,6 +9,7 @@ OFFSET_COLUMNS = Q // 16
 EXPERT_GROUPS = 4
 GROUP = E // EXPERT_GROUPS
 GROUP_COLUMNS = GROUP * Q
+WARMING_MATMULS = 12
 
 BF16, F32, U16 = mybir.dt.bfloat16, mybir.dt.float32, mybir.dt.uint16
 GELU = mybir.ActivationFunctionType.Gelu_apprx_tanh
@@ -37,6 +38,12 @@ def tile_gather_matmul_kernel(tc, table, w, b, offs, out):
         bias = held.tile([P, OUT_BLOCKS], F32, name="bias")
         with nc.allow_non_contiguous_dma(reason="256 single float32 values, one to a partition"):
             nc.scalar.dma_start(bias[:], b.rearrange("(a p) o -> p (a o)", p=P))
+
+        zeros = held.tile([P, P], BF16, name="zeros")
+        nc.vector.memset(zeros[:], 0.0)
+        unread = psum.tile([P, P], F32, name="unread")
+        for turn in range(WARMING_MATMULS):
+            nc.tensor.matmul(unread[:], zeros[:], zeros[:], start=True, stop=True)
 
         scratch = held.tile([P, 1], F32, name="scratch")
         nc.vector.memset(scratch[:], 0.0)

@@ -24,11 +24,11 @@ def tile_gather_matmul_kernel(tc, table, w, b, offs, out):
         tc.psum_pool(name="psum", bufs=1) as psum,
         tc.psum_pool(name="products", bufs=4) as products,
     ):
+        tokens = held.tile([P, TOKEN_BLOCKS, K], BF16, name="tokens")
+        nc.sync.dma_start(tokens[:], table.rearrange("(t p) k -> p t k", p=P))
+
         offsets = held.tile([P, N // 16], U16, name="offsets")
         nc.sync.dma_start(offsets[:], offs)
-
-        tokens = held.tile([P, TOKEN_BLOCKS, K], BF16, name="tokens")
-        nc.scalar.dma_start(tokens[:], table.rearrange("(t p) k -> p t k", p=P))
 
         weights = [held.tile([P, GROUP, M], BF16, name=f"weights{g}") for g in range(EXPERT_GROUPS)]
         w_by_k = w.rearrange("e k m -> k e m")

@@ -52,11 +52,10 @@ def tile_gather_matmul_kernel(tc, table, w, b, offs, out):
         identity = held.tile([P, P], BF16, name="identity")
         make_identity(nc, identity[:])
         window = held.tile([P, S], BF16, name="window")
-        flipped = [psum.tile([P, P], BF16, name=f"flipped{t}") for t in range(TOKEN_BLOCKS)]
+        flipped = psum.tile([P, S], BF16, name="flipped")
         for t in range(TOKEN_BLOCKS):
-            nc.tensor.transpose(flipped[t][:], tokens[:, t, :], identity[:])
-        nc.vector.tensor_copy(window[:, 0:P], flipped[0][:])
-        nc.scalar.copy(window[:, P:S], flipped[1][:])
+            nc.tensor.transpose(flipped[:, t * P : (t + 1) * P], tokens[:, t, :], identity[:])
+        nc.vector.tensor_copy(window[:], flipped[:])
 
         for g in range(EXPERT_GROUPS):
             for a in range(OUT_BLOCKS):

@@ -9,6 +9,7 @@ OFFSET_COLUMNS = Q // 16
 EXPERT_GROUPS = 4
 GROUP = E // EXPERT_GROUPS
 GROUP_COLUMNS = GROUP * Q
+PRODUCT_BANKS = 6
 WARMING_MATMULS = 12
 
 BF16, F32, U16 = mybir.dt.bfloat16, mybir.dt.float32, mybir.dt.uint16
@@ -22,7 +23,7 @@ def tile_gather_matmul_kernel(tc, table, w, b, offs, out):
     with (
         tc.tile_pool(name="held", bufs=1) as held,
         tc.psum_pool(name="psum", bufs=1) as psum,
-        tc.psum_pool(name="products", bufs=4) as products,
+        tc.psum_pool(name="products", bufs=PRODUCT_BANKS) as products,
     ):
         tokens = held.tile([P, TOKEN_BLOCKS, K], BF16, name="tokens")
         nc.sync.dma_start(tokens[:], table.rearrange("(t p) k -> p t k", p=P))

@@ -26,7 +26,8 @@ def tile_gather_matmul_kernel(tc, table, w, b, offs, out):
         tc.psum_pool(name="products", bufs=PRODUCT_BANKS) as products,
     ):
         tokens = held.tile([P, TOKEN_BLOCKS, K], BF16, name="tokens")
-        nc.sync.dma_start(tokens[:], table.rearrange("(t p) k -> p t k", p=P))
+        nc.sync.dma_start(tokens[:, 0, :], table[0:P, :])
+        nc.scalar.dma_start(tokens[:, 1, :], table[P:S, :])
 
         offsets = held.tile([P, N // 16], U16, name="offsets")
         nc.sync.dma_start(offsets[:], offs)

@@ -10,7 +10,8 @@ EXPERT_GROUPS = 4
 GROUP = E // EXPERT_GROUPS
 GROUP_COLUMNS = GROUP * Q
 PRODUCT_BANKS = 6
-WARMING_MATMULS = 12
+WARMING_MATMULS = 10
+BRIDGING_MATMULS = 2
 
 BF16, F32, U16 = mybir.dt.bfloat16, mybir.dt.float32, mybir.dt.uint16
 GELU = mybir.ActivationFunctionType.Gelu_apprx_tanh
@@ -58,6 +59,9 @@ def tile_gather_matmul_kernel(tc, table, w, b, offs, out):
         for t in range(TOKEN_BLOCKS):
             nc.tensor.transpose(flipped[:, t * P : (t + 1) * P], tokens[:, t, :], identity[:])
         nc.vector.tensor_copy(window[:], flipped[:])
+
+        for turn in range(BRIDGING_MATMULS):
+            nc.tensor.matmul(unread[:], identity[:], tokens[:, TOKEN_BLOCKS - 1, :], start=True, stop=True)
 
         for g in range(EXPERT_GROUPS):
             for a in range(OUT_BLOCKS):

@@ -23,7 +23,7 @@ def tile_gather_matmul_kernel(tc, table, w, b, offs, out):
     nc = tc.nc
     with (
         tc.tile_pool(name="held", bufs=1) as held,
-        tc.psum_pool(name="psum", bufs=1) as psum,
+        tc.psum_pool(name="flips", bufs=TOKEN_BLOCKS) as flips,
         tc.psum_pool(name="products", bufs=PRODUCT_BANKS) as products,
     ):
         tokens = held.tile([P, TOKEN_BLOCKS, K], BF16, name="tokens")
@@ -44,7 +44,7 @@ def tile_gather_matmul_kernel(tc, table, w, b, offs, out):
 
         zeros = held.tile([P, P], BF16, name="zeros")
         nc.vector.memset(zeros[:], 0.0)
-        unread = psum.tile([P, P], F32, name="unread")
+        unread = products.tile([P, P], F32, name="unread", tag="y")
         for turn in range(WARMING_MATMULS):
             nc.tensor.matmul(unread[:], zeros[:], zeros[:], start=True, stop=True)
 
@@ -55,17 +55,17 @@ def tile_gather_matmul_kernel(tc, table, w, b, offs, out):
         identity = held.tile([P, P], BF16, name="identity")
         make_identity(nc, identity[:])
         window = held.tile([P, S], BF16, name="window")
-        flipped = psum.tile([P, S], BF16, name="flipped")
         for t in range(TOKEN_BLOCKS):
-            nc.tensor.transpose(flipped[:, t * P : (t + 1) * P], tokens[:, t, :], identity[:])
-        nc.vector.tensor_copy(window[:], flipped[:])
+            flipped = flips.tile([P, P], BF16, name=f"flipped{t}", tag="flipped")
+            nc.tensor.transpose(flipped[:], tokens[:, t, :], identity[:])
+            nc.vector.tensor_copy(window[:, t * P : (t + 1) * P], flipped[:])
 
         for turn in range(BRIDGING_MATMULS):
             nc.tensor.matmul(unread[:], identity[:], tokens[:, TOKEN_BLOCKS - 1, :], start=True, stop=True)
 
         for g in range(EXPERT_GROUPS):
             for a in range(OUT_BLOCKS):
-                y = products.tile([P, GROUP_COLUMNS], F32, name="y")
+                y = products.tile([P, GROUP_COLUMNS], F32, name="y", tag="y")
                 for i in range(GROUP):
                     e = g * GROUP + i
                     nc.tensor.matmul(

@@ -1,5 +1,4 @@
 import concourse.mybir as mybir
-from concourse.masks import make_identity
 
 P = 128
 S, K, M, N, E, Q = 256, 128, 256, 512, 8, 64
@@ -42,18 +41,26 @@ def tile_gather_matmul_kernel(tc, table, w, b, offs, out):
         with nc.allow_non_contiguous_dma(reason="256 single float32 values, one to a partition"):
             nc.scalar.dma_start(bias[:], b.rearrange("(a p) o -> p (a o)", p=P))
 
-        zeros = held.tile([P, P], BF16, name="zeros")
-        nc.vector.memset(zeros[:], 0.0)
+        ones = held.tile([P, P], BF16, name="ones")
+        nc.vector.memset(ones[:], 1.0)
         unread = products.tile([P, P], F32, name="unread", tag="y")
         for turn in range(WARMING_MATMULS):
-            nc.tensor.matmul(unread[:], zeros[:], zeros[:], start=True, stop=True)
+            nc.tensor.matmul(unread[:], ones[:], ones[:], start=True, stop=True)
 
         scratch = held.tile([P, 1], F32, name="scratch")
         nc.vector.memset(scratch[:], 0.0)
         nc.scalar.activation(scratch[:], scratch[:], GELU)
 
         identity = held.tile([P, P], BF16, name="identity")
-        make_identity(nc, identity[:])
+        nc.gpsimd.affine_select(
+            out=identity[:],
+            in_=ones[:],
+            pattern=[[-1, P]],
+            compare_op=mybir.AluOpType.is_equal,
+            fill=0.0,
+            base=0,
+            channel_multiplier=1,
+        )
         window = held.tile([P, S], BF16, name="window")
         for t in range(TOKEN_BLOCKS):
             flipped = flips.tile([P, P], BF16, name=f"flipped{t}", tag="flipped")

@@ -10,7 +10,7 @@ GROUP = E // EXPERT_GROUPS
 GROUP_COLUMNS = GROUP * Q
 PRODUCT_BANKS = 6
 WARMING_MATMULS = 10
-BRIDGING_MATMULS = 2
+BRIDGING_MATMULS = 4
 
 BF16, F32, U16 = mybir.dt.bfloat16, mybir.dt.float32, mybir.dt.uint16
 GELU = mybir.ActivationFunctionType.Gelu_apprx_tanh
@@ -29,12 +29,14 @@ def tile_gather_matmul_kernel(tc, table, w, b, offs, out):
         nc.sync.dma_start(tokens[:, 0, :], table[0:P, :])
         nc.scalar.dma_start(tokens[:, 1, :], table[P:S, :])
 
+        weights = [held.tile([P, GROUP, M], BF16, name=f"weights{g}") for g in range(EXPERT_GROUPS)]
+        w_by_k = w.rearrange("e k m -> k e m")
+        nc.sync.dma_start(weights[0][:], w_by_k[:, 0:GROUP, :])
+
         offsets = held.tile([P, N // 16], U16, name="offsets")
         nc.sync.dma_start(offsets[:], offs)
 
-        weights = [held.tile([P, GROUP, M], BF16, name=f"weights{g}") for g in range(EXPERT_GROUPS)]
-        w_by_k = w.rearrange("e k m -> k e m")
-        for g in range(EXPERT_GROUPS):
+        for g in range(1, EXPERT_GROUPS):
             nc.sync.dma_start(weights[g][:], w_by_k[:, g * GROUP : (g + 1) * GROUP, :])
 
         bias = held.tile([P, OUT_BLOCKS], F32, name="bias")

import concourse.mybir as mybir

P = 128
S, K, M, N, E, Q = 256, 128, 256, 512, 8, 64
TOKEN_BLOCKS = S // P
OUT_BLOCKS = M // P
OFFSET_COLUMNS = Q // 16
EXPERT_GROUPS = 4
GROUP = E // EXPERT_GROUPS
GROUP_COLUMNS = GROUP * Q
PRODUCT_BANKS = 6
WARMING_MATMULS = 10
BRIDGING_MATMULS = 4

BF16, F32, U16 = mybir.dt.bfloat16, mybir.dt.float32, mybir.dt.uint16
GELU = mybir.ActivationFunctionType.Gelu_apprx_tanh

FLOPS = 2 * K * M * N


def tile_gather_matmul_kernel(tc, table, w, b, offs, out):
    nc = tc.nc
    with (
        tc.tile_pool(name="held", bufs=1) as held,
        tc.psum_pool(name="flips", bufs=TOKEN_BLOCKS) as flips,
        tc.psum_pool(name="products", bufs=PRODUCT_BANKS) as products,
    ):
        tokens = held.tile([P, TOKEN_BLOCKS, K], BF16, name="tokens")
        nc.sync.dma_start(tokens[:, 0, :], table[0:P, :])
        nc.scalar.dma_start(tokens[:, 1, :], table[P:S, :])

        weights = [held.tile([P, GROUP, M], BF16, name=f"weights{g}") for g in range(EXPERT_GROUPS)]
        w_by_k = w.rearrange("e k m -> k e m")
        nc.sync.dma_start(weights[0][:], w_by_k[:, 0:GROUP, :])

        offsets = held.tile([P, N // 16], U16, name="offsets")
        nc.sync.dma_start(offsets[:], offs)

        for g in range(1, EXPERT_GROUPS):
            nc.sync.dma_start(weights[g][:], w_by_k[:, g * GROUP : (g + 1) * GROUP, :])

        bias = held.tile([P, OUT_BLOCKS], F32, name="bias")
        with nc.allow_non_contiguous_dma(reason="256 single float32 values, one to a partition"):
            nc.scalar.dma_start(bias[:], b.rearrange("(a p) o -> p (a o)", p=P))

        ones = held.tile([P, P], BF16, name="ones")
        nc.vector.memset(ones[:], 1.0)
        unread = products.tile([P, P], F32, name="unread", tag="y")
        for turn in range(WARMING_MATMULS):
            nc.tensor.matmul(unread[:], ones[:], ones[:], start=True, stop=True)

        scratch = held.tile([P, 1], F32, name="scratch")
        nc.vector.memset(scratch[:], 0.0)
        nc.scalar.activation(scratch[:], scratch[:], GELU)

        identity = held.tile([P, P], BF16, name="identity")
        nc.gpsimd.affine_select(
            out=identity[:],
            in_=ones[:],
            pattern=[[-1, P]],
            compare_op=mybir.AluOpType.is_equal,
            fill=0.0,
            base=0,
            channel_multiplier=1,
        )
        window = held.tile([P, S], BF16, name="window")
        for t in range(TOKEN_BLOCKS):
            flipped = flips.tile([P, P], BF16, name=f"flipped{t}", tag="flipped")
            nc.tensor.transpose(flipped[:], tokens[:, t, :], identity[:])
            nc.vector.tensor_copy(window[:, t * P : (t + 1) * P], flipped[:])

        for turn in range(BRIDGING_MATMULS):
            nc.tensor.matmul(unread[:], identity[:], tokens[:, TOKEN_BLOCKS - 1, :], start=True, stop=True)

        for g in range(EXPERT_GROUPS):
            for a in range(OUT_BLOCKS):
                y = products.tile([P, GROUP_COLUMNS], F32, name="y", tag="y")
                for i in range(GROUP):
                    e = g * GROUP + i
                    nc.tensor.matmul(
                        y[:, i * Q : (i + 1) * Q],
                        weights[g][:, i, a * P : (a + 1) * P],
                        window[:].indirect(offsets[:, e * OFFSET_COLUMNS : (e + 1) * OFFSET_COLUMNS]),
                        start=True,
                        stop=True,
                    )
                result = held.tile([P, GROUP_COLUMNS], F32, name=f"result{g}{a}")
                nc.scalar.activation(result[:], y[:], GELU, bias=bias[:, a : a + 1])
                nc.sync.dma_start(
                    out[a * P : (a + 1) * P, g * GROUP_COLUMNS : (g + 1) * GROUP_COLUMNS], result[:]
                )
